import numpy as np
import ml_dtypes


def mxq(x, axis, fmt="e4m3"):
    dtype, down = {"e4m3": (ml_dtypes.float8_e4m3fn, 7), "e5m2": (ml_dtypes.float8_e5m2, 14)}[fmt]
    v = np.moveaxis(np.asarray(x, np.float32).astype(ml_dtypes.bfloat16).astype(np.float64), axis, -1)
    blocks = v.reshape(v.shape[:-1] + (-1, 32))
    amax = np.abs(blocks).max(-1, keepdims=True)
    byte = np.maximum(np.where(amax > 0, np.frexp(amax)[1] - 1 + 127, 0) - down, 1)
    scale = np.exp2(byte - 127.0)
    codes = (blocks / scale).astype(np.float32).astype(dtype).astype(np.float64)
    return np.moveaxis((codes * scale).reshape(v.shape), -1, axis)


WIDE = False


def mx_kscale(k):
    if not WIDE:
        return np.ones(k)
    levels = np.array([10, -10, 5, -5, 0])
    if k % 512:
        return np.exp2(np.random.permutation(np.resize(levels, k // 32))).repeat(32)
    a = np.empty((k // 512, 16))
    for p in range(k // 512):
        a[p, :8] = np.random.permutation(np.resize(levels, 8))
        for g in range(8):
            far = levels[np.abs(levels - a[p, g]) >= 10]
            a[p, g + 8] = far[np.random.randint(len(far))]
    return np.exp2(a.ravel()).repeat(32)


BF16 = ml_dtypes.bfloat16


def bf(x):
    return np.asarray(x, np.float32).astype(BF16)


def f64(x):
    return np.asarray(x).astype(np.float64)


B, N, G, F, C = 32, 8, 512, 1024, 1024

GAMMA = 10.0
CUTOFF = 5.0


def shifted_softplus(t):
    return np.logaddexp(t, 0.0) - np.log(2.0)


def gaussian_basis(dist, mu):
    diff = dist[..., None] - mu
    return np.exp(-GAMMA * np.square(diff))


def cosine_cutoff(dist):
    return 0.5 * (np.cos(np.pi * dist / CUTOFF) + 1.0)


def draw0():
    s, t = mx_kscale(G), mx_kscale(F)
    return {
        "x": bf(np.random.standard_normal((B, N, C))),
        "dist": bf(np.random.uniform(0.5, 4.5, (B, N, N))),
        "mu": bf(np.random.uniform(0.0, 5.0, G)),
        "gr": bf(np.random.standard_normal(G) * s),
        "w1": bf(np.random.standard_normal((G, F)) * 5.0 / np.sqrt(G) / s[:, None]),
        "gf": bf((1.0 + 0.1 * np.random.standard_normal(F)) * t),
        "w2": bf(np.random.standard_normal((F, C)) * 1.5 / np.sqrt(F) / t[:, None]),
    }


def core(x, dist, mu, gr, w1, gf, w2):
    x, dist = f64(x), f64(dist)
    n = x.shape[1]
    rbf = gaussian_basis(dist, f64(mu))
    r = (rbf * f64(gr)).reshape(-1, G)
    h = mxq(r, 1, "e4m3") @ mxq(f64(w1), 0, "e4m3")
    f1 = shifted_softplus(h) * f64(gf)
    filt = mxq(f1, 1, "e4m3") @ mxq(f64(w2), 0, "e4m3")
    filt = filt.reshape(dist.shape + (C,))
    fc = cosine_cutoff(dist)
    messages = x[:, None, :, :] * fc[..., None] * filt
    return np.sum(messages, axis=2) / np.sqrt(n)


def e4m3fn_bytes(y):
    return np.clip(np.asarray(y, np.float64), -448.0, 448.0).astype(np.float32).astype(ml_dtypes.float8_e4m3fn).view(np.uint8)


def e4m3fn_values(b):
    return np.asarray(b, np.uint8).view(ml_dtypes.float8_e4m3fn).astype(np.float64)


def setup_inputs():
    d = draw0()
    x0 = np.asarray(d['w2']).astype(np.float64)
    s = (np.max(np.abs(x0), axis=(1,), keepdims=True) / 448.0).astype(np.float32)
    out = {}
    for k, v in d.items():
        if k == 'w2':
            out['w2_bytes'] = e4m3fn_bytes(x0 / s.astype(np.float64))
            out['w2_scale'] = s
        else:
            out[k] = v
    return out


def reference(x, dist, mu, gr, w1, gf, w2_bytes, w2_scale):
    return core(x, dist, mu, gr, w1, gf, e4m3fn_values(w2_bytes) * w2_scale.astype(np.float64))

@@ -1,0 +1,483 @@
+import math
+from contextlib import ExitStack
+
+import concourse.mybir as mybir
+from concourse.masks import make_identity
+
+B, N, G, F, C = 32, 8, 512, 1024, 1024
+FLOPS = 2 * B * N * N * (G * F + F * C)
+
+F32 = mybir.dt.float32
+BF16 = mybir.dt.bfloat16
+I32 = mybir.dt.int32
+U32 = mybir.dt.uint32
+U8 = mybir.dt.uint8
+FP8 = mybir.dt.float8_e4m3fn
+FP8X4 = mybir.dt.float8_e4m3fn_x4
+ALU = mybir.AluOpType
+ACT = mybir.ActivationFunctionType
+ENG = mybir.EngineType
+
+P = 128
+PACK = 4
+BANK = 512
+TILES = 16
+TERMS = 8
+CHUNKS = [6,6,4]
+TINY = 2.0 ** -60
+STARTS = [-30,6,34]
+SCALAR_PLANES = 2
+POOL_CYCLE = [1]
+POOL_TILES = 15
+
+
+def tile_schnetfilterinteraction_kernel(tc, x, dist, mu, gr, w1, gf, w2_bytes, w2_scale, out):
+    nc = tc.nc
+    with ExitStack() as ctx:
+        keep = ctx.enter_context(tc.tile_pool(name="keep", bufs=1))
+        work = ctx.enter_context(tc.tile_pool(name="work", bufs=2))
+        psum = ctx.enter_context(tc.psum_pool(name="psum", bufs=2))
+        ctx.enter_context(tc.manual_schedule())
+
+        gr_sb = keep.tile([P, PACK], BF16, name="gr_sb")
+        nc.sync.dma_start(out=gr_sb[:], in_=gr.rearrange("(p t) -> p t", t=PACK))
+        mu_sb = keep.tile([P, PACK], BF16, name="mu_sb")
+        nc.sync.dma_start(out=mu_sb[:], in_=mu.rearrange("(p t) -> p t", t=PACK))
+        d_sb = keep.tile([P, TILES], BF16, name="d_sb")
+        dist_q = dist.rearrange("b (h q) j -> q b h j", q=4)
+        for q in range(4):
+            nc.sync.dma_start(out=d_sb[32 * q : 32 * q + 32, :].rearrange("p (h j) -> p h j", j=N), in_=dist_q[q])
+        w2s_sb = keep.tile([P, 2, PACK], F32, name="w2s_sb")
+        nc.sync.dma_start(out=w2s_sb[:], in_=w2_scale.rearrange("(g p t) o -> p g (t o)", p=P, t=PACK))
+        w2_rows = w2_bytes.rearrange("(g p t) c -> g p (t c)", p=P, t=PACK)
+        w1_rows = w1.rearrange("(p t) f -> p t f", t=PACK)
+        w2_raw = [keep.tile([P, PACK * C], U8, name="w2_fp8_bytes%d" % g) for g in range(2)]
+        w1_raw = [keep.tile([P, PACK, BANK], BF16, name="w1_raw%d" % g) for g in range(2)]
+        nc.sync.dma_start(out=w2_raw[0][:], in_=w2_rows[0])
+        for g in range(2):
+            nc.sync.dma_start(out=w1_raw[g][:], in_=w1_rows[:, :, g * BANK : (g + 1) * BANK])
+        nc.sync.dma_start(out=w2_raw[1][:], in_=w2_rows[1])
+        gf_sb = keep.tile([P, 2, PACK], BF16, name="gf_sb")
+        nc.sync.dma_start(out=gf_sb[:], in_=gf.rearrange("(g p t) -> p g t", p=P, t=PACK))
+        x_sb = keep.tile([P, N * C], BF16, name="x_sb")
+        for q in range(4):
+            nc.sync.dma_start(out=x_sb[32 * q : 32 * q + 32, :], in_=x.rearrange("b j c -> b (j c)"))
+
+        ident_bf = keep.tile([P, P], BF16, name="ident_bf")
+        make_identity(nc, ident_bf[:])
+        ident_f = keep.tile([P, P], F32, name="ident_f")
+        make_identity(nc, ident_f[:])
+
+        tiny = keep.tile([P, 1], F32, name="tiny")
+        nc.vector.memset(tiny[:], TINY)
+        pair_terms = keep.tile([P, TILES * TERMS + P], BF16, name="pair_terms")
+        nc.vector.memset(pair_terms[:], 1.0)
+        gauss_terms = keep.tile([P, PACK, P], BF16, name="gauss_terms")
+        nc.vector.memset(gauss_terms[:], 0.0)
+        nc.vector.memset(gauss_terms[:, :, 1:3], 1.0)
+
+        gr_abs = keep.tile([P, PACK], F32, name="gr_abs")
+        nc.vector.scalar_tensor_tensor(out=gr_abs[:], in0=gr_sb[:], scalar=-1.0, in1=gr_sb[:], op0=ALU.mult, op1=ALU.max)
+        gr_log = keep.tile([P, PACK], F32, name="gr_log")
+        nc.scalar.activation(out=gr_log[:], in_=gr_abs[:], func=ACT.Ln, bias=tiny[:])
+
+        floor = keep.tile([P, 1], F32, name="floor")
+        nc.scalar.activation(out=floor[:], in_=tiny[:], func=ACT.Exp, bias=-42.0)
+        wide0 = keep.tile([P, PACK, C], BF16, name="wide0")
+        for t in range(SCALAR_PLANES):
+            nc.scalar.activation(
+                out=wide0[:, t, :], in_=w2_raw[0][:, t * C : (t + 1) * C].bitcast(FP8), func=ACT.Copy, scale=w2s_sb[:, 0, t : t + 1]
+            )
+
+        pt = pair_terms[:, 0 : TILES * TERMS].rearrange("p (a k) -> p a k", k=TERMS)
+        mu_sq = keep.tile([P, PACK], F32, name="mu_sq")
+        d_sq = keep.tile([P, TILES], F32, name="d_sq")
+        nc.vector.tensor_tensor(out=mu_sq[:], in0=mu_sb[:], in1=mu_sb[:], op=ALU.mult)
+        nc.vector.tensor_scalar(out=gauss_terms[:, :, 0], in0=mu_sb[:], scalar1=-2.0, scalar2=None, op0=ALU.mult)
+        nc.vector.tensor_tensor(out=d_sq[:], in0=d_sb[:], in1=d_sb[:], op=ALU.mult)
+        nc.vector.tensor_copy(out=gauss_terms[:, :, 3], in_=mu_sq[:])
+        nc.vector.tensor_copy(out=pt[:, :, 0], in_=d_sb[:])
+        nc.vector.tensor_copy(out=pt[:, :, 1], in_=d_sq[:])
+        nc.vector.tensor_tensor(out=gauss_terms[:, :, 4], in0=mu_sq[:], in1=gauss_terms[:, :, 3], op=ALU.subtract)
+        nc.vector.tensor_scalar(out=gauss_terms[:, :, 5], in0=gr_log[:], scalar1=-0.1, scalar2=None, op0=ALU.mult)
+        nc.vector.tensor_tensor(out=pt[:, :, 2], in0=d_sq[:], in1=pt[:, :, 1], op=ALU.subtract)
+        log_rest = keep.tile([P, PACK], F32, name="log_rest")
+        nc.vector.scalar_tensor_tensor(
+            out=log_rest[:], in0=gr_log[:], scalar=-0.1, in1=gauss_terms[:, :, 5], op0=ALU.mult, op1=ALU.subtract
+        )
+        gr_neg = keep.tile([P, PACK], F32, name="gr_neg")
+        nc.vector.tensor_scalar(out=gr_neg[:], in0=gr_sb[:], scalar1=0.0, scalar2=2.0, op0=ALU.is_lt, op1=ALU.mult)
+        nc.vector.tensor_copy(out=gauss_terms[:, :, 6], in_=log_rest[:])
+        minus_sign = keep.tile([P, PACK], F32, name="minus_sign")
+        nc.vector.tensor_scalar(out=minus_sign[:], in0=gr_neg[:], scalar1=-1.0, scalar2=None, op0=ALU.add)
+        nc.vector.tensor_tensor(out=gauss_terms[:, :, 7], in0=log_rest[:], in1=gauss_terms[:, :, 6], op=ALU.subtract)
+
+        pair_rows = keep.tile([P, TILES * P], BF16, name="pair_rows")
+        gauss_rows = keep.tile([P, PACK * P], BF16, name="gauss_rows")
+
+        def turn_pairs(half):
+            turned = psum.tile([P, 8 * P], BF16, name="turned", tag="sums")
+            for a in range(8):
+                first = (8 * half + a) * TERMS
+                nc.tensor.transpose(turned[:, a * P : (a + 1) * P], pair_terms[:, first : first + P], ident_bf[:])
+            nc.vector.tensor_copy(out=pair_rows[:, half * 8 * P : (half + 1) * 8 * P], in_=turned[:])
+
+        turn_pairs(0)
+        turned_g = psum.tile([P, PACK * P], BF16, name="turned_g", tag="again")
+        for t in range(PACK):
+            nc.tensor.transpose(turned_g[:, t * P : (t + 1) * P], gauss_terms[:, t, :], ident_bf[:])
+        nc.vector.tensor_copy(out=gauss_rows[:], in_=turned_g[:])
+
+        fc = keep.tile([P, TILES], F32, name="fc")
+        u = keep.tile([P, TILES], F32, name="u")
+        whole = keep.tile([P, TILES], I32, name="whole")
+        ang = keep.tile([P, TILES], F32, name="ang")
+        ang2 = keep.tile([P, TILES], F32, name="ang2")
+        poly = keep.tile([P, TILES], F32, name="poly")
+        small = [
+            lambda: nc.vector.tensor_scalar(out=u[:], in0=d_sb[:], scalar1=0.1, scalar2=None, op0=ALU.mult),
+            lambda: nc.vector.tensor_copy(out=whole[:], in_=u[:]),
+            lambda: nc.vector.tensor_tensor(out=u[:], in0=u[:], in1=whole[:], op=ALU.subtract),
+            lambda: nc.vector.scalar_tensor_tensor(out=u[:], in0=u[:], scalar=-1.0, in1=u[:], op0=ALU.mult, op1=ALU.max),
+            lambda: nc.vector.tensor_scalar(
+                out=ang[:], in0=u[:], scalar1=-math.pi, scalar2=math.pi / 2, op0=ALU.mult, op1=ALU.add
+            ),
+            lambda: nc.vector.tensor_tensor(out=ang2[:], in0=ang[:], in1=ang[:], op=ALU.mult),
+            lambda: nc.vector.tensor_scalar(
+                out=poly[:], in0=ang2[:], scalar1=-1.0 / math.factorial(15), scalar2=None, op0=ALU.mult
+            ),
+        ]
+
+        def horner(k):
+            coef = (-1.0) ** k / math.factorial(2 * k + 1)
+            other = ang2 if k > 0 else ang
+            return lambda: nc.vector.scalar_tensor_tensor(
+                out=poly[:], in0=poly[:], scalar=coef, in1=other[:], op0=ALU.add, op1=ALU.mult
+            )
+
+        small.extend(horner(k) for k in range(6, -1, -1))
+        small.append(
+            lambda: nc.vector.scalar_tensor_tensor(
+                out=fc[:], in0=poly[:], scalar=1.0 / math.sqrt(N), in1=poly[:], op0=ALU.mult, op1=ALU.mult
+            )
+        )
+        minus_gf = keep.tile([P, 2, PACK], F32, name="minus_gf")
+        small.append(
+            lambda: nc.vector.tensor_scalar(out=minus_gf[:], in0=gf_sb[:], scalar1=-1.0, scalar2=None, op0=ALU.mult)
+        )
+
+        w1_codes = keep.tile([P, F], U32, name="w1_codes", align_bytes=64)
+        w1_scales = keep.tile([P, F], U8, name="w1_scales", align_bytes=64)
+        w2_codes = keep.tile([P, 2, C], U32, name="w2_codes", align_bytes=64)
+        w2_scales = keep.tile([P, 2, C], U8, name="w2_scales", align_bytes=64)
+
+        def w1_sign(g):
+            signed = work.tile([P, PACK, BANK], BF16, name="signed", tag="signed")
+            for j in range(PACK):
+                nc.vector.tensor_scalar(
+                    out=signed[:, j, :], in0=w1_raw[g][:, j, :], scalar1=minus_sign[:, j : j + 1], scalar2=None, op0=ALU.mult
+                )
+            return signed
+
+        def w1_group(signed):
+            grouped = work.tile([P, PACK * BANK], BF16, name="grouped", tag="grouped", align_bytes=64)
+            nc.vector.tensor_copy(
+                out=grouped[:].rearrange("p (t a e j) -> p a t e j", t=PACK, e=2, j=PACK),
+                in_=signed[:].rearrange("p j (a e t) -> p a t e j", t=PACK, e=2),
+            )
+            return grouped
+
+        def w1_quantize(g, grouped):
+            cols = slice(g * BANK, (g + 1) * BANK)
+            nc.vector.quantize_mx(out=w1_codes[:, cols].bitcast(FP8X4), scales=w1_scales[:, cols], in_=grouped[:])
+
+        wide1 = keep.tile([P, PACK, C], BF16, name="wide1")
+        wide = [wide0, wide1]
+
+        def w2_widen(g, t):
+            nc.vector.tensor_scalar(
+                out=wide[g][:, t, :], in0=w2_raw[g][:, t * C : (t + 1) * C].bitcast(FP8), scalar1=w2s_sb[:, g, t : t + 1],
+                scalar2=None, op0=ALU.mult,
+            )
+
+        def w2_group(g, half):
+            grouped = work.tile([P, PACK * BANK], BF16, name="grouped", tag="grouped", align_bytes=64)
+            nc.vector.tensor_copy(
+                out=grouped[:].rearrange("p (a e t) -> p a t e", t=PACK, e=4),
+                in_=wide[g][:, :, half * BANK : (half + 1) * BANK].rearrange("p t (a e) -> p a t e", e=4),
+            )
+            return grouped
+
+        def w2_quantize(g, half, grouped):
+            cols = slice(half * BANK, (half + 1) * BANK)
+            nc.vector.quantize_mx(out=w2_codes[:, g, cols].bitcast(FP8X4), scales=w2_scales[:, g, cols], in_=grouped[:])
+
+        signed0 = w1_sign(0)
+        turn_pairs(1)
+        r_codes = keep.tile([P, TILES * P], U32, name="r_codes", align_bytes=64)
+        r_scales = keep.tile([P, TILES * P], U8, name="r_scales", align_bytes=64)
+        r_bf = []
+        for quad in range(4):
+            rb = keep.tile([P, 4 * BANK], BF16, name="r_bf%d" % quad, align_bytes=64)
+            r_bf.append(rb)
+            for a in range(4):
+                tl = 4 * quad + a
+                expo = psum.tile([P, PACK, P], F32, name="expo", tag=("first", "filt")[tl % 2])
+                for t in range(PACK):
+                    nc.tensor.matmul(
+                        expo[:, t, :],
+                        lhsT=gauss_rows[:, t * P : (t + 1) * P],
+                        rhs=pair_rows[:, tl * P : (tl + 1) * P],
+                        start=True,
+                        stop=True,
+                    )
+                nc.scalar.activation(
+                    out=rb[:, a * BANK : (a + 1) * BANK].rearrange("p (n t) -> p n t", t=PACK),
+                    in_=expo[:].rearrange("p t n -> p n t"),
+                    func=ACT.Exp,
+                    scale=-10.0,
+                )
+
+        def quantize_r(quad):
+            cols = slice(quad * BANK, (quad + 1) * BANK)
+            nc.vector.quantize_mx(out=r_codes[:, cols].bitcast(FP8X4), scales=r_scales[:, cols], in_=r_bf[quad][:])
+
+
+        small[0]()
+        grouped0 = w1_group(signed0)
+        small[1]()
+        signed1 = w1_sign(1)
+        small[2]()
+        w1_quantize(0, grouped0)
+        small[3]()
+        grouped1 = w1_group(signed1)
+        small[4]()
+        quantize_r(0)
+        small[5]()
+        w1_quantize(1, grouped1)
+        small[6]()
+        for t in range(SCALAR_PLANES, PACK):
+            w2_widen(0, t)
+        small[7]()
+        for t in range(PACK):
+            w2_widen(1, t)
+            small[8 + t]()
+        for quarter in range(4):
+            half, g = divmod(quarter, 2)
+            grouped = w2_group(g, half)
+            small[12 + quarter]()
+            if quarter < 3:
+                quantize_r(quarter + 1)
+            w2_quantize(g, half, grouped)
+
+        def hidden(tl, g, tag):
+            bank = psum.tile([P, PACK, P], F32, name="hidden", tag=tag)
+            pairs = slice(tl * P, (tl + 1) * P)
+            for t in range(PACK):
+                cols = slice(g * BANK + t * P, g * BANK + (t + 1) * P)
+                nc.tensor.matmul_mx(
+                    out=bank[:, t, :],
+                    lhsT=w1_codes[:, cols].bitcast(FP8X4),
+                    lhsT_scale=w1_scales[:, cols],
+                    rhs=r_codes[:, pairs].bitcast(FP8X4),
+                    rhs_scale=r_scales[:, pairs],
+                    start=True,
+                    stop=True,
+                )
+            return bank[:].rearrange("p t n -> p n t")
+
+        logs = {}
+        soft = {}
+        f1 = {}
+        filt = {}
+        msg = {}
+        sums = {}
+        back = {}
+
+        def sigmoid(bank):
+            tl, g = divmod(bank, 2)
+            if g == 0:
+                logs[tl] = keep.tile([P, 2, P, PACK], F32, name="logs%d" % tl)
+            nc.scalar.activation(out=logs[tl][:, g, :, :], in_=hidden(tl, g, "first"), func=ACT.Sigmoid)
+
+        def logarithm(tl):
+            flat = logs[tl][:].rearrange("p g n t -> p (g n t)")
+            nc.scalar.activation(out=flat, in_=flat, func=ACT.Ln, scale=2.0, bias=floor[:])
+
+        again = {}
+
+        def recompute(tl):
+            again[tl] = []
+            for g in range(2):
+                again[tl].append(hidden(tl, g, "again"))
+                slot()
+
+        def guard(tl):
+            y = work.tile([P, 2, P, PACK], F32, name="soft", tag="soft", bufs=3)
+            soft[tl] = y
+            for g in range(2):
+                nc.vector.scalar_tensor_tensor(
+                    out=y[:, g, :, :], in0=again[tl][g], scalar=math.log(2.0), in1=logs[tl][:, g, :, :], op0=ALU.add, op1=ALU.min
+                )
+
+        def gain(tl, pooled, first, last):
+            if first < last:
+                engine = nc.gpsimd if pooled else nc.vector
+                f = work.tile(
+                    [P, last - first, P, PACK], BF16, name="f1", tag="f1_pool" if pooled else "f1_vector", align_bytes=64,
+                    bufs=1 if pooled else 2,
+                )
+                f1.setdefault(tl, []).append((first, last, f))
+                engine.tensor_tensor(
+                    out=f[:],
+                    in0=soft[tl][:, first:last, :, :],
+                    in1=minus_gf[:, first:last, :].unsqueeze(2).to_broadcast([P, last - first, P, PACK]),
+                    op=ALU.mult,
+                )
+
+        def filters(tl):
+            codes = work.tile([P, 2 * P], U32, name="f1_codes", tag="f1_codes", align_bytes=64)
+            scales = work.tile([P, 2 * P], U8, name="f1_scales", tag="f1_scales", align_bytes=64)
+            for first, last, f in f1[tl]:
+                nc.vector.quantize_mx(
+                    out=codes[:, first * P : last * P].bitcast(FP8X4),
+                    scales=scales[:, first * P : last * P],
+                    in_=f[:].rearrange("p g n t -> p (g n t)"),
+                )
+            return codes, scales
+
+        def second_product(tl, codes, scales):
+            filt[tl] = []
+            for half in range(2):
+                cols = slice(half * BANK, (half + 1) * BANK)
+                bank = psum.tile([P, BANK], F32, name="filt", tag="filt")
+                for g in range(2):
+                    nc.tensor.matmul_mx(
+                        out=bank[:],
+                        lhsT=codes[:, g * P : (g + 1) * P].bitcast(FP8X4),
+                        lhsT_scale=scales[:, g * P : (g + 1) * P],
+                        rhs=w2_codes[:, g, cols].bitcast(FP8X4),
+                        rhs_scale=w2_scales[:, g, cols],
+                        start=(g == 0),
+                        stop=(g == 1),
+                    )
+                filt[tl].append(bank)
+                slot()
+
+        def messages(tl):
+            j = tl % N
+            msg[tl] = []
+            for half in range(2):
+                m = work.tile([P, BANK], F32, name="msg", tag="msg", bufs=12)
+                first = j * C + half * BANK
+                nc.vector.scalar_tensor_tensor(
+                    out=m[:], in0=filt[tl][half][:], scalar=fc[:, tl : tl + 1], in1=x_sb[:, first : first + BANK],
+                    op0=ALU.mult, op1=ALU.mult,
+                )
+                msg[tl].append(m)
+
+        def add_up(tl):
+            h, j = divmod(tl, N)
+            if j == 0:
+                sums[h] = [psum.tile([P, BANK], F32, name="sums", tag="sums") for half in range(2)]
+            for half in range(2):
+                for a in range(4):
+                    nc.tensor.matmul(
+                        sums[h][half][:, a * P : (a + 1) * P],
+                        lhsT=msg[tl][half][:, a * P : (a + 1) * P],
+                        rhs=ident_f[:],
+                        is_transpose=True,
+                        start=(j == 0 and a == 0),
+                        stop=(j == N - 2 and a == 3),
+                    )
+
+        def turn_back(h):
+            back[h] = []
+            parked = []
+            for half in range(2):
+                sb = work.tile([P, BANK], F32, name="parked", tag="parked")
+                nc.scalar.copy(out=sb[:], in_=sums[h][half][:])
+                parked.append(sb)
+            for half in range(2):
+                bank = psum.tile([P, BANK], F32, name="back", tag="sums")
+                for a in range(4):
+                    nc.tensor.transpose(bank[:, a * P : (a + 1) * P], parked[half][:, a * P : (a + 1) * P], ident_f[:])
+                back[h].append(bank)
+
+        out_q = out.rearrange("b (h q) c -> h q b c", q=4)
+
+        def finish(h):
+            for half in range(2):
+                res = work.tile([P, BANK], F32, name="res", tag="res")
+                nc.vector.tensor_tensor(out=res[:], in0=back[h][half][:], in1=msg[N * h + N - 1][half][:], op=ALU.add)
+                for q in range(4):
+                    queue = nc.scalar if h == 1 and q % 2 else nc.sync
+                    queue.dma_start(
+                        out=out_q[h, q][:, half * BANK : (half + 1) * BANK], in_=res[32 * q : 32 * q + 32, :]
+                    )
+
+        plan = []
+        first = 0
+        for c, size in enumerate(CHUNKS):
+            for bank in range(2 * first, 2 * (first + size)):
+                plan.append((STARTS[c] + bank - 2 * first, bank, first if bank == 2 * (first + size) - 1 else None))
+            first += size
+        busy = set(when for when, bank, since in plan)
+        clock = [STARTS[0]]
+
+        def slot():
+            for when, bank, since in plan:
+                if when == clock[0]:
+                    sigmoid(bank)
+                    if since is not None:
+                        for tl in range(since, bank // 2 + 1):
+                            logarithm(tl)
+            clock[0] = clock[0] + 1
+
+        waiting = []
+        stage = {0: "adding", 1: "waiting"}
+
+        def sums_step(k, calm):
+            for h in range(2):
+                if stage[h] == "turned" and N * h + N - 1 in msg:
+                    finish(h)
+                    stage[h] = "done"
+                    stage[1] = "adding" if h == 0 else "done"
+                elif stage[h] == "added":
+                    turn_back(h)
+                    stage[h] = "turned"
+                elif stage[h] == "adding" and calm:
+                    for tl in [tl for tl in waiting if tl // N == h][:2]:
+                        add_up(tl)
+                        waiting.remove(tl)
+                        if tl % N == N - 2:
+                            stage[h] = "added"
+
+        def step(k):
+            a, q, m = k - 1, k - 2, k - 3
+            share = POOL_CYCLE[a % len(POOL_CYCLE)] if a < POOL_TILES else 0
+            if 0 <= a < TILES:
+                gain(a, False, share, 2)
+            if 0 <= q < TILES:
+                quantized = filters(q)
+            if 0 <= a < TILES:
+                gain(a, True, 0, share)
+            if k < TILES:
+                guard(k)
+            calm = clock[0] not in busy and clock[0] + 4 not in busy
+            if k + 1 < TILES:
+                recompute(k + 1)
+            if 0 <= m < TILES:
+                messages(m)
+                if m % N < N - 1:
+                    waiting.append(m)
+            if 0 <= q < TILES:
+                second_product(q, *quantized)
+            sums_step(k, calm)
+            slot()
+
+        for early in range(-STARTS[0] - 2):
+            slot()
+        recompute(0)
+        for k in range(TILES + 4):
+            step(k)

@@ -16,19 +16,19 @@ FP8 = mybir.dt.float8_e4m3fn
 FP8X4 = mybir.dt.float8_e4m3fn_x4
 ALU = mybir.AluOpType
 ACT = mybir.ActivationFunctionType
-ENG = mybir.EngineType
 
 P = 128
 PACK = 4
 BANK = 512
-TILES = 16
+TILES = B * N * N // P
+QUADS = 4
 TERMS = 8
+SLOTS = 5
+
 CHUNKS = [6,6,4]
-TINY = 2.0 ** -60
-STARTS = [-30,6,34]
-SCALAR_PLANES = 2
-POOL_CYCLE = [1]
-POOL_TILES = 15
+CHUNK_SLOTS = [10,41]
+GPSIMD_WORDS = 192
+SCALAR_ROWS = 2
 
 
 def tile_schnetfilterinteraction_kernel(tc, x, dist, mu, gr, w1, gf, w2_bytes, w2_scale, out):
@@ -43,12 +43,12 @@ def tile_schnetfilterinteraction_kernel(tc, x, dist, mu, gr, w1, gf, w2_bytes, w
         nc.sync.dma_start(out=gr_sb[:], in_=gr.rearrange("(p t) -> p t", t=PACK))
         mu_sb = keep.tile([P, PACK], BF16, name="mu_sb")
         nc.sync.dma_start(out=mu_sb[:], in_=mu.rearrange("(p t) -> p t", t=PACK))
-        d_sb = keep.tile([P, TILES], BF16, name="d_sb")
-        dist_q = dist.rearrange("b (h q) j -> q b h j", q=4)
-        for q in range(4):
-            nc.sync.dma_start(out=d_sb[32 * q : 32 * q + 32, :].rearrange("p (h j) -> p h j", j=N), in_=dist_q[q])
-        w2s_sb = keep.tile([P, 2, PACK], F32, name="w2s_sb")
-        nc.sync.dma_start(out=w2s_sb[:], in_=w2_scale.rearrange("(g p t) o -> p g (t o)", p=P, t=PACK))
+        dist_sb = keep.tile([P, TILES], BF16, name="dist_sb")
+        dist_q = dist.rearrange("b (h q) j -> q b h j", q=QUADS)
+        for q in range(QUADS):
+            nc.sync.dma_start(out=dist_sb[B * q : B * (q + 1), :].rearrange("p (h j) -> p h j", j=N), in_=dist_q[q])
+        w2_scale_sb = keep.tile([P, 2, PACK], F32, name="w2_scale_sb")
+        nc.sync.dma_start(out=w2_scale_sb[:], in_=w2_scale.rearrange("(g p t) o -> p g (t o)", p=P, t=PACK))
         w2_rows = w2_bytes.rearrange("(g p t) c -> g p (t c)", p=P, t=PACK)
         w1_rows = w1.rearrange("(p t) f -> p t f", t=PACK)
         w2_raw = [keep.tile([P, PACK * C], U8, name="w2_fp8_bytes%d" % g) for g in range(2)]
@@ -60,16 +60,16 @@ def tile_schnetfilterinteraction_kernel(tc, x, dist, mu, gr, w1, gf, w2_bytes, w
         gf_sb = keep.tile([P, 2, PACK], BF16, name="gf_sb")
         nc.sync.dma_start(out=gf_sb[:], in_=gf.rearrange("(g p t) -> p g t", p=P, t=PACK))
         x_sb = keep.tile([P, N * C], BF16, name="x_sb")
-        for q in range(4):
-            nc.sync.dma_start(out=x_sb[32 * q : 32 * q + 32, :], in_=x.rearrange("b j c -> b (j c)"))
+        for q in range(QUADS):
+            nc.sync.dma_start(out=x_sb[B * q : B * (q + 1), :], in_=x.rearrange("b j c -> b (j c)"))
 
         ident_bf = keep.tile([P, P], BF16, name="ident_bf")
         make_identity(nc, ident_bf[:])
-        ident_f = keep.tile([P, P], F32, name="ident_f")
-        make_identity(nc, ident_f[:])
+        ident_f32 = keep.tile([P, P], F32, name="ident_f32")
+        make_identity(nc, ident_f32[:])
 
         tiny = keep.tile([P, 1], F32, name="tiny")
-        nc.vector.memset(tiny[:], TINY)
+        nc.vector.memset(tiny[:], 2.0**-60)
         pair_terms = keep.tile([P, TILES * TERMS + P], BF16, name="pair_terms")
         nc.vector.memset(pair_terms[:], 1.0)
         gauss_terms = keep.tile([P, PACK, P], BF16, name="gauss_terms")
@@ -80,98 +80,125 @@ def tile_schnetfilterinteraction_kernel(tc, x, dist, mu, gr, w1, gf, w2_bytes, w
         nc.vector.scalar_tensor_tensor(out=gr_abs[:], in0=gr_sb[:], scalar=-1.0, in1=gr_sb[:], op0=ALU.mult, op1=ALU.max)
         gr_log = keep.tile([P, PACK], F32, name="gr_log")
         nc.scalar.activation(out=gr_log[:], in_=gr_abs[:], func=ACT.Ln, bias=tiny[:])
-
         floor = keep.tile([P, 1], F32, name="floor")
         nc.scalar.activation(out=floor[:], in_=tiny[:], func=ACT.Exp, bias=-42.0)
-        wide0 = keep.tile([P, PACK, C], BF16, name="wide0")
-        for t in range(SCALAR_PLANES):
+        w2_wide = [keep.tile([P, PACK, C], BF16, name="w2_wide%d" % g) for g in range(2)]
+        for t in range(SCALAR_ROWS):
             nc.scalar.activation(
-                out=wide0[:, t, :], in_=w2_raw[0][:, t * C : (t + 1) * C].bitcast(FP8), func=ACT.Copy, scale=w2s_sb[:, 0, t : t + 1]
+                out=w2_wide[0][:, t, :],
+                in_=w2_raw[0][:, t * C : (t + 1) * C].bitcast(FP8),
+                func=ACT.Copy,
+                scale=w2_scale_sb[:, 0, t : t + 1],
             )
 
-        pt = pair_terms[:, 0 : TILES * TERMS].rearrange("p (a k) -> p a k", k=TERMS)
+        pair_term = pair_terms[:, 0 : TILES * TERMS].rearrange("p (a k) -> p a k", k=TERMS)
         mu_sq = keep.tile([P, PACK], F32, name="mu_sq")
-        d_sq = keep.tile([P, TILES], F32, name="d_sq")
+        dist_sq = keep.tile([P, TILES], F32, name="dist_sq")
+        log_rest = keep.tile([P, PACK], F32, name="log_rest")
+        gr_negative = keep.tile([P, PACK], F32, name="gr_negative")
+        minus_sign = keep.tile([P, PACK], F32, name="minus_sign")
         nc.vector.tensor_tensor(out=mu_sq[:], in0=mu_sb[:], in1=mu_sb[:], op=ALU.mult)
         nc.vector.tensor_scalar(out=gauss_terms[:, :, 0], in0=mu_sb[:], scalar1=-2.0, scalar2=None, op0=ALU.mult)
-        nc.vector.tensor_tensor(out=d_sq[:], in0=d_sb[:], in1=d_sb[:], op=ALU.mult)
-        nc.vector.tensor_copy(out=gauss_terms[:, :, 3], in_=mu_sq[:])
-        nc.vector.tensor_copy(out=pt[:, :, 0], in_=d_sb[:])
-        nc.vector.tensor_copy(out=pt[:, :, 1], in_=d_sq[:])
-        nc.vector.tensor_tensor(out=gauss_terms[:, :, 4], in0=mu_sq[:], in1=gauss_terms[:, :, 3], op=ALU.subtract)
+        nc.vector.tensor_tensor(out=dist_sq[:], in0=dist_sb[:], in1=dist_sb[:], op=ALU.mult)
+        nc.vector.tensor_copy(out=pair_term[:, :, 0], in_=dist_sb[:])
         nc.vector.tensor_scalar(out=gauss_terms[:, :, 5], in0=gr_log[:], scalar1=-0.1, scalar2=None, op0=ALU.mult)
-        nc.vector.tensor_tensor(out=pt[:, :, 2], in0=d_sq[:], in1=pt[:, :, 1], op=ALU.subtract)
-        log_rest = keep.tile([P, PACK], F32, name="log_rest")
+        nc.vector.tensor_copy(out=pair_term[:, :, 1], in_=dist_sq[:])
         nc.vector.scalar_tensor_tensor(
             out=log_rest[:], in0=gr_log[:], scalar=-0.1, in1=gauss_terms[:, :, 5], op0=ALU.mult, op1=ALU.subtract
         )
-        gr_neg = keep.tile([P, PACK], F32, name="gr_neg")
-        nc.vector.tensor_scalar(out=gr_neg[:], in0=gr_sb[:], scalar1=0.0, scalar2=2.0, op0=ALU.is_lt, op1=ALU.mult)
+        nc.vector.tensor_tensor(out=pair_term[:, :, 2], in0=dist_sq[:], in1=pair_term[:, :, 1], op=ALU.subtract)
         nc.vector.tensor_copy(out=gauss_terms[:, :, 6], in_=log_rest[:])
-        minus_sign = keep.tile([P, PACK], F32, name="minus_sign")
-        nc.vector.tensor_scalar(out=minus_sign[:], in0=gr_neg[:], scalar1=-1.0, scalar2=None, op0=ALU.add)
+        nc.vector.tensor_scalar(out=gr_negative[:], in0=gr_sb[:], scalar1=0.0, scalar2=2.0, op0=ALU.is_lt, op1=ALU.mult)
+        nc.vector.tensor_copy(out=gauss_terms[:, :, 3], in_=mu_sq[:])
         nc.vector.tensor_tensor(out=gauss_terms[:, :, 7], in0=log_rest[:], in1=gauss_terms[:, :, 6], op=ALU.subtract)
+        nc.vector.tensor_scalar(out=minus_sign[:], in0=gr_negative[:], scalar1=-1.0, scalar2=None, op0=ALU.add)
+        nc.vector.tensor_tensor(out=gauss_terms[:, :, 4], in0=mu_sq[:], in1=gauss_terms[:, :, 3], op=ALU.subtract)
 
         pair_rows = keep.tile([P, TILES * P], BF16, name="pair_rows")
         gauss_rows = keep.tile([P, PACK * P], BF16, name="gauss_rows")
 
-        def turn_pairs(half):
-            turned = psum.tile([P, 8 * P], BF16, name="turned", tag="sums")
-            for a in range(8):
-                first = (8 * half + a) * TERMS
-                nc.tensor.transpose(turned[:, a * P : (a + 1) * P], pair_terms[:, first : first + P], ident_bf[:])
-            nc.vector.tensor_copy(out=pair_rows[:, half * 8 * P : (half + 1) * 8 * P], in_=turned[:])
+        def turn_pairs(first, last):
+            turned = psum.tile([P, (last - first) * P], BF16, name="turned", tag="sums")
+            for a in range(first, last):
+                nc.tensor.transpose(
+                    turned[:, (a - first) * P : (a - first + 1) * P], pair_terms[:, a * TERMS : a * TERMS + P], ident_bf[:]
+                )
+            return lambda: nc.vector.tensor_copy(out=pair_rows[:, first * P : last * P], in_=turned[:])
 
-        turn_pairs(0)
-        turned_g = psum.tile([P, PACK * P], BF16, name="turned_g", tag="again")
-        for t in range(PACK):
-            nc.tensor.transpose(turned_g[:, t * P : (t + 1) * P], gauss_terms[:, t, :], ident_bf[:])
-        nc.vector.tensor_copy(out=gauss_rows[:], in_=turned_g[:])
+        def turn_gaussians():
+            turned = psum.tile([P, PACK * P], BF16, name="turned", tag="guard")
+            for t in range(PACK):
+                nc.tensor.transpose(turned[:, t * P : (t + 1) * P], gauss_terms[:, t, :], ident_bf[:])
+            nc.vector.tensor_copy(out=gauss_rows[:], in_=turned[:])
 
-        fc = keep.tile([P, TILES], F32, name="fc")
-        u = keep.tile([P, TILES], F32, name="u")
+        r_codes = keep.tile([P, TILES * P], U32, name="r_codes", align_bytes=64)
+        r_scales = keep.tile([P, TILES * P], U8, name="r_scales", align_bytes=64)
+        r_bf = [keep.tile([P, 4 * BANK], BF16, name="r_bf%d" % n, align_bytes=64) for n in range(TILES // 4)]
+
+        def radial_basis(tl):
+            expo = psum.tile([P, PACK, P], F32, name="expo", tag=("sigmoid", "filt")[tl % 2])
+            for t in range(PACK):
+                nc.tensor.matmul(
+                    expo[:, t, :],
+                    lhsT=gauss_rows[:, t * P : (t + 1) * P],
+                    rhs=pair_rows[:, tl * P : (tl + 1) * P],
+                    start=True,
+                    stop=True,
+                )
+            place = slice(tl % 4 * BANK, (tl % 4 + 1) * BANK)
+            nc.scalar.activation(
+                out=r_bf[tl // 4][:, place].rearrange("p (n t) -> p n t", t=PACK),
+                in_=expo[:].rearrange("p t n -> p n t"),
+                func=ACT.Exp,
+                scale=-10.0,
+            )
+
+        def quantize_r(n):
+            cols = slice(n * BANK, (n + 1) * BANK)
+            nc.vector.quantize_mx(out=r_codes[:, cols].bitcast(FP8X4), scales=r_scales[:, cols], in_=r_bf[n][:])
+
+        cutoff = keep.tile([P, TILES], F32, name="cutoff")
+        turns = keep.tile([P, TILES], F32, name="turns")
         whole = keep.tile([P, TILES], I32, name="whole")
-        ang = keep.tile([P, TILES], F32, name="ang")
-        ang2 = keep.tile([P, TILES], F32, name="ang2")
-        poly = keep.tile([P, TILES], F32, name="poly")
-        small = [
-            lambda: nc.vector.tensor_scalar(out=u[:], in0=d_sb[:], scalar1=0.1, scalar2=None, op0=ALU.mult),
-            lambda: nc.vector.tensor_copy(out=whole[:], in_=u[:]),
-            lambda: nc.vector.tensor_tensor(out=u[:], in0=u[:], in1=whole[:], op=ALU.subtract),
-            lambda: nc.vector.scalar_tensor_tensor(out=u[:], in0=u[:], scalar=-1.0, in1=u[:], op0=ALU.mult, op1=ALU.max),
-            lambda: nc.vector.tensor_scalar(
-                out=ang[:], in0=u[:], scalar1=-math.pi, scalar2=math.pi / 2, op0=ALU.mult, op1=ALU.add
-            ),
-            lambda: nc.vector.tensor_tensor(out=ang2[:], in0=ang[:], in1=ang[:], op=ALU.mult),
-            lambda: nc.vector.tensor_scalar(
-                out=poly[:], in0=ang2[:], scalar1=-1.0 / math.factorial(15), scalar2=None, op0=ALU.mult
-            ),
-        ]
+        angle = keep.tile([P, TILES], F32, name="angle")
+        angle_sq = keep.tile([P, TILES], F32, name="angle_sq")
+        sine = keep.tile([P, TILES], F32, name="sine")
 
         def horner(k):
-            coef = (-1.0) ** k / math.factorial(2 * k + 1)
-            other = ang2 if k > 0 else ang
+            factor = angle_sq if k > 0 else angle
             return lambda: nc.vector.scalar_tensor_tensor(
-                out=poly[:], in0=poly[:], scalar=coef, in1=other[:], op0=ALU.add, op1=ALU.mult
+                out=sine[:], in0=sine[:], scalar=(-1.0) ** k / math.factorial(2 * k + 1), in1=factor[:], op0=ALU.add, op1=ALU.mult
             )
 
-        small.extend(horner(k) for k in range(6, -1, -1))
-        small.append(
+        cutoff_steps = [
+            lambda: nc.vector.tensor_scalar(out=turns[:], in0=dist_sb[:], scalar1=0.1, scalar2=None, op0=ALU.mult),
+            lambda: nc.vector.tensor_copy(out=whole[:], in_=turns[:]),
+            lambda: nc.vector.tensor_tensor(out=turns[:], in0=turns[:], in1=whole[:], op=ALU.subtract),
             lambda: nc.vector.scalar_tensor_tensor(
-                out=fc[:], in0=poly[:], scalar=1.0 / math.sqrt(N), in1=poly[:], op0=ALU.mult, op1=ALU.mult
+                out=turns[:], in0=turns[:], scalar=-1.0, in1=turns[:], op0=ALU.mult, op1=ALU.max
+            ),
+            lambda: nc.vector.tensor_scalar(
+                out=angle[:], in0=turns[:], scalar1=-math.pi, scalar2=math.pi / 2, op0=ALU.mult, op1=ALU.add
+            ),
+            lambda: nc.vector.tensor_tensor(out=angle_sq[:], in0=angle[:], in1=angle[:], op=ALU.mult),
+            lambda: nc.vector.tensor_scalar(
+                out=sine[:], in0=angle_sq[:], scalar1=-1.0 / math.factorial(15), scalar2=None, op0=ALU.mult
+            ),
+        ]
+        cutoff_steps.extend(horner(k) for k in range(6, -1, -1))
+        cutoff_steps.append(
+            lambda: nc.vector.scalar_tensor_tensor(
+                out=cutoff[:], in0=sine[:], scalar=1.0 / math.sqrt(N), in1=sine[:], op0=ALU.mult, op1=ALU.mult
             )
-        )
-        minus_gf = keep.tile([P, 2, PACK], F32, name="minus_gf")
-        small.append(
-            lambda: nc.vector.tensor_scalar(out=minus_gf[:], in0=gf_sb[:], scalar1=-1.0, scalar2=None, op0=ALU.mult)
         )
 
         w1_codes = keep.tile([P, F], U32, name="w1_codes", align_bytes=64)
         w1_scales = keep.tile([P, F], U8, name="w1_scales", align_bytes=64)
         w2_codes = keep.tile([P, 2, C], U32, name="w2_codes", align_bytes=64)
         w2_scales = keep.tile([P, 2, C], U8, name="w2_scales", align_bytes=64)
+        minus_gf = keep.tile([P, 2, P, PACK], F32, name="minus_gf")
 
-        def w1_sign(g):
+        def sign_w1(g):
             signed = work.tile([P, PACK, BANK], BF16, name="signed", tag="signed")
             for j in range(PACK):
                 nc.vector.tensor_scalar(
@@ -179,7 +206,7 @@ def tile_schnetfilterinteraction_kernel(tc, x, dist, mu, gr, w1, gf, w2_bytes, w
                 )
             return signed
 
-        def w1_group(signed):
+        def group_w1(signed):
             grouped = work.tile([P, PACK * BANK], BF16, name="grouped", tag="grouped", align_bytes=64)
             nc.vector.tensor_copy(
                 out=grouped[:].rearrange("p (t a e j) -> p a t e j", t=PACK, e=2, j=PACK),
@@ -187,91 +214,81 @@ def tile_schnetfilterinteraction_kernel(tc, x, dist, mu, gr, w1, gf, w2_bytes, w
             )
             return grouped
 
-        def w1_quantize(g, grouped):
+        def quantize_w1(g, grouped):
             cols = slice(g * BANK, (g + 1) * BANK)
             nc.vector.quantize_mx(out=w1_codes[:, cols].bitcast(FP8X4), scales=w1_scales[:, cols], in_=grouped[:])
 
-        wide1 = keep.tile([P, PACK, C], BF16, name="wide1")
-        wide = [wide0, wide1]
-
-        def w2_widen(g, t):
+        def widen_w2(g, t):
             nc.vector.tensor_scalar(
-                out=wide[g][:, t, :], in0=w2_raw[g][:, t * C : (t + 1) * C].bitcast(FP8), scalar1=w2s_sb[:, g, t : t + 1],
-                scalar2=None, op0=ALU.mult,
+                out=w2_wide[g][:, t, :],
+                in0=w2_raw[g][:, t * C : (t + 1) * C].bitcast(FP8),
+                scalar1=w2_scale_sb[:, g, t : t + 1],
+                scalar2=None,
+                op0=ALU.mult,
             )
 
-        def w2_group(g, half):
+        def group_w2(g, half):
             grouped = work.tile([P, PACK * BANK], BF16, name="grouped", tag="grouped", align_bytes=64)
             nc.vector.tensor_copy(
                 out=grouped[:].rearrange("p (a e t) -> p a t e", t=PACK, e=4),
-                in_=wide[g][:, :, half * BANK : (half + 1) * BANK].rearrange("p t (a e) -> p a t e", e=4),
+                in_=w2_wide[g][:, :, half * BANK : (half + 1) * BANK].rearrange("p t (a e) -> p a t e", e=4),
             )
             return grouped
 
-        def w2_quantize(g, half, grouped):
+        def quantize_w2(g, half, grouped):
             cols = slice(half * BANK, (half + 1) * BANK)
             nc.vector.quantize_mx(out=w2_codes[:, g, cols].bitcast(FP8X4), scales=w2_scales[:, g, cols], in_=grouped[:])
 
-        signed0 = w1_sign(0)
-        turn_pairs(1)
-        r_codes = keep.tile([P, TILES * P], U32, name="r_codes", align_bytes=64)
-        r_scales = keep.tile([P, TILES * P], U8, name="r_scales", align_bytes=64)
-        r_bf = []
-        for quad in range(4):
-            rb = keep.tile([P, 4 * BANK], BF16, name="r_bf%d" % quad, align_bytes=64)
-            r_bf.append(rb)
-            for a in range(4):
-                tl = 4 * quad + a
-                expo = psum.tile([P, PACK, P], F32, name="expo", tag=("first", "filt")[tl % 2])
-                for t in range(PACK):
-                    nc.tensor.matmul(
-                        expo[:, t, :],
-                        lhsT=gauss_rows[:, t * P : (t + 1) * P],
-                        rhs=pair_rows[:, tl * P : (tl + 1) * P],
-                        start=True,
-                        stop=True,
-                    )
-                nc.scalar.activation(
-                    out=rb[:, a * BANK : (a + 1) * BANK].rearrange("p (n t) -> p n t", t=PACK),
-                    in_=expo[:].rearrange("p t n -> p n t"),
-                    func=ACT.Exp,
-                    scale=-10.0,
-                )
+        turn_pairs(0, 4)()
+        copy_pairs = turn_pairs(4, 8)
+        turn_gaussians()
+        copy_pairs()
+        radial_basis(0)
+        radial_basis(1)
+        copy_pairs = turn_pairs(8, TILES)
+        signed = sign_w1(0)
+        copy_pairs()
+        for tl in range(2, TILES):
+            radial_basis(tl)
 
-        def quantize_r(quad):
-            cols = slice(quad * BANK, (quad + 1) * BANK)
-            nc.vector.quantize_mx(out=r_codes[:, cols].bitcast(FP8X4), scales=r_scales[:, cols], in_=r_bf[quad][:])
-
-
-        small[0]()
-        grouped0 = w1_group(signed0)
-        small[1]()
-        signed1 = w1_sign(1)
-        small[2]()
-        w1_quantize(0, grouped0)
-        small[3]()
-        grouped1 = w1_group(signed1)
-        small[4]()
-        quantize_r(0)
-        small[5]()
-        w1_quantize(1, grouped1)
-        small[6]()
-        for t in range(SCALAR_PLANES, PACK):
-            w2_widen(0, t)
-        small[7]()
+        long_steps = []
+        grouped = {}
+        long_steps.append(lambda: grouped.setdefault("w1a", group_w1(signed)))
+        long_steps.append(lambda: grouped.setdefault("signed", sign_w1(1)))
+        long_steps.append(lambda: quantize_w1(0, grouped["w1a"]))
+        long_steps.append(lambda: grouped.setdefault("w1b", group_w1(grouped["signed"])))
+        long_steps.append(lambda: quantize_r(0))
+        long_steps.append(lambda: quantize_w1(1, grouped["w1b"]))
+        for step_no, long_step in enumerate(long_steps):
+            cutoff_steps[step_no]()
+            long_step()
+        cutoff_steps[6]()
+        for t in range(SCALAR_ROWS, PACK):
+            widen_w2(0, t)
+        quantize_r(1)
         for t in range(PACK):
-            w2_widen(1, t)
-            small[8 + t]()
+            cutoff_steps[7 + t]()
+            widen_w2(1, t)
+        between = [
+            lambda: quantize_r(2),
+            lambda: quantize_r(3),
+            lambda: nc.vector.tensor_scalar(
+                out=minus_gf[:], in0=gf_sb[:].unsqueeze(2).to_broadcast([P, 2, P, PACK]), scalar1=-1.0, scalar2=None, op0=ALU.mult
+            ),
+            cutoff_steps[14],
+        ]
         for quarter in range(4):
             half, g = divmod(quarter, 2)
-            grouped = w2_group(g, half)
-            small[12 + quarter]()
+            ready = group_w2(g, half)
             if quarter < 3:
-                quantize_r(quarter + 1)
-            w2_quantize(g, half, grouped)
+                cutoff_steps[11 + quarter]()
+            between[quarter]()
+            quantize_w2(g, half, ready)
 
-        def hidden(tl, g, tag):
-            bank = psum.tile([P, PACK, P], F32, name="hidden", tag=tag)
+        logs, again, soft, f1, filt, msg, sums, back = {}, {}, {}, {}, {}, {}, {}, {}
+
+        def minus_h(tl, g, tag):
+            bank = psum.tile([P, PACK, P], F32, name="minus_h", tag=tag)
             pairs = slice(tl * P, (tl + 1) * P)
             for t in range(PACK):
                 cols = slice(g * BANK + t * P, g * BANK + (t + 1) * P)
@@ -286,71 +303,75 @@ def tile_schnetfilterinteraction_kernel(tc, x, dist, mu, gr, w1, gf, w2_bytes, w
                 )
             return bank[:].rearrange("p t n -> p n t")
 
-        logs = {}
-        soft = {}
-        f1 = {}
-        filt = {}
-        msg = {}
-        sums = {}
-        back = {}
-
-        def sigmoid(bank):
-            tl, g = divmod(bank, 2)
+        def sigmoid(tl, g, tag):
             if g == 0:
-                logs[tl] = keep.tile([P, 2, P, PACK], F32, name="logs%d" % tl)
-            nc.scalar.activation(out=logs[tl][:, g, :, :], in_=hidden(tl, g, "first"), func=ACT.Sigmoid)
+                logs[tl] = work.tile([P, 2, P, PACK], F32, name="logs", tag="logs", bufs=CHUNKS[0] + CHUNKS[1])
+            nc.scalar.activation(out=logs[tl][:, g, :, :], in_=minus_h(tl, g, tag), func=ACT.Sigmoid)
 
         def logarithm(tl):
             flat = logs[tl][:].rearrange("p g n t -> p (g n t)")
             nc.scalar.activation(out=flat, in_=flat, func=ACT.Ln, scale=2.0, bias=floor[:])
 
-        again = {}
-
         def recompute(tl):
             again[tl] = []
             for g in range(2):
-                again[tl].append(hidden(tl, g, "again"))
+                again[tl].append(minus_h(tl, g, "guard"))
                 slot()
 
         def guard(tl):
-            y = work.tile([P, 2, P, PACK], F32, name="soft", tag="soft", bufs=3)
-            soft[tl] = y
+            soft[tl] = work.tile([P, 2, P, PACK], F32, name="soft", tag="soft", bufs=3)
             for g in range(2):
                 nc.vector.scalar_tensor_tensor(
-                    out=y[:, g, :, :], in0=again[tl][g], scalar=math.log(2.0), in1=logs[tl][:, g, :, :], op0=ALU.add, op1=ALU.min
+                    out=soft[tl][:, g, :, :],
+                    in0=again[tl][g],
+                    scalar=math.log(2.0),
+                    in1=logs[tl][:, g, :, :],
+                    op0=ALU.add,
+                    op1=ALU.min,
                 )
 
-        def gain(tl, pooled, first, last):
-            if first < last:
-                engine = nc.gpsimd if pooled else nc.vector
-                f = work.tile(
-                    [P, last - first, P, PACK], BF16, name="f1", tag="f1_pool" if pooled else "f1_vector", align_bytes=64,
-                    bufs=1 if pooled else 2,
-                )
-                f1.setdefault(tl, []).append((first, last, f))
-                engine.tensor_tensor(
-                    out=f[:],
-                    in0=soft[tl][:, first:last, :, :],
-                    in1=minus_gf[:, first:last, :].unsqueeze(2).to_broadcast([P, last - first, P, PACK]),
-                    op=ALU.mult,
-                )
+        def gain(tl, engine, first, last):
+            part = work.tile(
+                [P, (last - first) * PACK], BF16, name="f1", tag="f1_from%d" % min(first, 1), align_bytes=64,
+                bufs=1 if first == 0 else 3,
+            )
+            f1.setdefault(tl, []).append((first, last, part))
+            cols = slice(first * PACK, last * PACK)
+            engine.tensor_tensor(
+                out=part[:],
+                in0=soft[tl][:].rearrange("p g n t -> p (g n t)")[:, cols],
+                in1=minus_gf[:].rearrange("p g n t -> p (g n t)")[:, cols],
+                op=ALU.mult,
+            )
 
-        def filters(tl):
-            codes = work.tile([P, 2 * P], U32, name="f1_codes", tag="f1_codes", align_bytes=64)
-            scales = work.tile([P, 2 * P], U8, name="f1_scales", tag="f1_scales", align_bytes=64)
-            for first, last, f in f1[tl]:
-                nc.vector.quantize_mx(
-                    out=codes[:, first * P : last * P].bitcast(FP8X4),
-                    scales=scales[:, first * P : last * P],
-                    in_=f[:].rearrange("p g n t -> p (g n t)"),
+        def gain_on_scalar(tl):
+            planes = work.tile([P, PACK, P], BF16, name="planes", tag="planes")
+            for t in range(PACK):
+                nc.scalar.activation(
+                    out=planes[:, t, :], in_=soft[tl][:, 1, :, t], func=ACT.Copy, scale=minus_gf[:, 1, 0, t : t + 1]
                 )
+            part = work.tile([P, BANK], BF16, name="f1", tag="f1_from1", align_bytes=64, bufs=3)
+            f1.setdefault(tl, []).append((P, 2 * P, part))
+            nc.scalar.copy(out=part[:].rearrange("p (n t) -> p n t", t=PACK), in_=planes[:].rearrange("p t n -> p n t"))
+
+        def quantize_f1(tl):
+            codes = work.tile([P, 2 * P], U32, name="f1_codes", tag="f1_codes", align_bytes=64, bufs=3)
+            scales = work.tile([P, 2 * P], U8, name="f1_scales", tag="f1_scales", align_bytes=64, bufs=3)
+            for first, last, part in f1[tl]:
+                cuts = [first, P, last] if first < P < last else [first, last]
+                for lo, hi in zip(cuts, cuts[1:]):
+                    nc.vector.quantize_mx(
+                        out=codes[:, lo:hi].bitcast(FP8X4),
+                        scales=scales[:, lo:hi],
+                        in_=part[:, (lo - first) * PACK : (hi - first) * PACK],
+                    )
             return codes, scales
 
-        def second_product(tl, codes, scales):
+        def second_product(tl, tag, codes, scales):
             filt[tl] = []
             for half in range(2):
                 cols = slice(half * BANK, (half + 1) * BANK)
-                bank = psum.tile([P, BANK], F32, name="filt", tag="filt")
+                bank = psum.tile([P, BANK], F32, name="filt", tag=tag)
                 for g in range(2):
                     nc.tensor.matmul_mx(
                         out=bank[:],
@@ -365,119 +386,129 @@ def tile_schnetfilterinteraction_kernel(tc, x, dist, mu, gr, w1, gf, w2_bytes, w
                 slot()
 
         def messages(tl):
-            j = tl % N
             msg[tl] = []
             for half in range(2):
-                m = work.tile([P, BANK], F32, name="msg", tag="msg", bufs=12)
-                first = j * C + half * BANK
+                part = work.tile([P, BANK], F32, name="msg", tag="msg", bufs=16)
+                first = tl % N * C + half * BANK
                 nc.vector.scalar_tensor_tensor(
-                    out=m[:], in0=filt[tl][half][:], scalar=fc[:, tl : tl + 1], in1=x_sb[:, first : first + BANK],
-                    op0=ALU.mult, op1=ALU.mult,
+                    out=part[:],
+                    in0=filt[tl][half][:],
+                    scalar=cutoff[:, tl : tl + 1],
+                    in1=x_sb[:, first : first + BANK],
+                    op0=ALU.mult,
+                    op1=ALU.mult,
                 )
-                msg[tl].append(m)
+                msg[tl].append(part)
+
+        added = [N - 1, N - 1]
 
         def add_up(tl):
             h, j = divmod(tl, N)
             if j == 0:
                 sums[h] = [psum.tile([P, BANK], F32, name="sums", tag="sums") for half in range(2)]
             for half in range(2):
-                for a in range(4):
+                for a in range(BANK // P):
                     nc.tensor.matmul(
                         sums[h][half][:, a * P : (a + 1) * P],
                         lhsT=msg[tl][half][:, a * P : (a + 1) * P],
-                        rhs=ident_f[:],
+                        rhs=ident_f32[:],
                         is_transpose=True,
                         start=(j == 0 and a == 0),
-                        stop=(j == N - 2 and a == 3),
+                        stop=(j == added[h] - 1 and a == BANK // P - 1),
                     )
 
         def turn_back(h):
-            back[h] = []
-            parked = []
+            parked = [work.tile([P, BANK], F32, name="parked", tag="parked") for half in range(2)]
             for half in range(2):
-                sb = work.tile([P, BANK], F32, name="parked", tag="parked")
-                nc.scalar.copy(out=sb[:], in_=sums[h][half][:])
-                parked.append(sb)
+                nc.scalar.copy(out=parked[half][:], in_=sums[h][half][:])
+            back[h] = []
             for half in range(2):
                 bank = psum.tile([P, BANK], F32, name="back", tag="sums")
-                for a in range(4):
-                    nc.tensor.transpose(bank[:, a * P : (a + 1) * P], parked[half][:, a * P : (a + 1) * P], ident_f[:])
+                for a in range(BANK // P):
+                    nc.tensor.transpose(bank[:, a * P : (a + 1) * P], parked[half][:, a * P : (a + 1) * P], ident_f32[:])
                 back[h].append(bank)
 
-        out_q = out.rearrange("b (h q) c -> h q b c", q=4)
+        out_q = out.rearrange("b (h q) c -> h q b c", q=QUADS)
 
-        def finish(h):
+        def add_on_vector(tl):
+            h, j = divmod(tl, N)
             for half in range(2):
-                res = work.tile([P, BANK], F32, name="res", tag="res")
-                nc.vector.tensor_tensor(out=res[:], in0=back[h][half][:], in1=msg[N * h + N - 1][half][:], op=ALU.add)
-                for q in range(4):
-                    queue = nc.scalar if h == 1 and q % 2 else nc.sync
-                    queue.dma_start(
-                        out=out_q[h, q][:, half * BANK : (half + 1) * BANK], in_=res[32 * q : 32 * q + 32, :]
-                    )
+                total = work.tile([P, BANK], F32, name="total", tag="total")
+                nc.vector.tensor_tensor(out=total[:], in0=back[h][half][:], in1=msg[tl][half][:], op=ALU.add)
+                back[h][half] = total
+                if j == N - 1:
+                    for q in range(QUADS):
+                        queue = nc.scalar if tl == TILES - 1 and q % 2 else nc.sync
+                        queue.dma_start(
+                            out=out_q[h, q][:, half * BANK : (half + 1) * BANK], in_=total[B * q : B * (q + 1), :]
+                        )
 
-        plan = []
-        first = 0
-        for c, size in enumerate(CHUNKS):
-            for bank in range(2 * first, 2 * (first + size)):
-                plan.append((STARTS[c] + bank - 2 * first, bank, first if bank == 2 * (first + size) - 1 else None))
-            first += size
-        busy = set(when for when, bank, since in plan)
-        clock = [STARTS[0]]
+        plan = {}
+        first = CHUNKS[0]
+        for size, start, tags in zip(CHUNKS[1:], CHUNK_SLOTS, (("sigmoid", "sums"), ("sigmoid", "sigmoid"))):
+            for n in range(2 * size):
+                plan[start + n] = (first + n // 2, n % 2, tags[n % 2], range(first, first + size) if n == 2 * size - 1 else [])
+            first = first + size
+        clock = [0]
 
         def slot():
-            for when, bank, since in plan:
-                if when == clock[0]:
-                    sigmoid(bank)
-                    if since is not None:
-                        for tl in range(since, bank // 2 + 1):
-                            logarithm(tl)
+            if clock[0] in plan:
+                tl, g, tag, finished = plan[clock[0]]
+                sigmoid(tl, g, tag)
+                for done in finished:
+                    logarithm(done)
             clock[0] = clock[0] + 1
 
-        waiting = []
-        stage = {0: "adding", 1: "waiting"}
+        next_sum = [0]
+        last_chunk = TILES - CHUNKS[-1]
 
-        def sums_step(k, calm):
-            for h in range(2):
-                if stage[h] == "turned" and N * h + N - 1 in msg:
-                    finish(h)
-                    stage[h] = "done"
-                    stage[1] = "adding" if h == 0 else "done"
-                elif stage[h] == "added":
-                    turn_back(h)
-                    stage[h] = "turned"
-                elif stage[h] == "adding" and calm:
-                    for tl in [tl for tl in waiting if tl // N == h][:2]:
+        def advance_sums(calm):
+            h, j = divmod(next_sum[0], N)
+            if j >= added[h] and h in back and next_sum[0] in msg:
+                add_on_vector(next_sum[0])
+                next_sum[0] = next_sum[0] + 1
+            elif j == added[h] and h not in back:
+                turn_back(h)
+            if calm:
+                h, j = divmod(next_sum[0], N)
+                for tl in range(next_sum[0], N * h + min(j + 2, added[min(h, 1)])):
+                    if tl in msg:
                         add_up(tl)
-                        waiting.remove(tl)
-                        if tl % N == N - 2:
-                            stage[h] = "added"
+                        next_sum[0] = tl + 1
+            if next_sum[0] == N + added[1] and 1 not in back:
+                turn_back(1)
 
-        def step(k):
-            a, q, m = k - 1, k - 2, k - 3
-            share = POOL_CYCLE[a % len(POOL_CYCLE)] if a < POOL_TILES else 0
-            if 0 <= a < TILES:
-                gain(a, False, share, 2)
-            if 0 <= q < TILES:
-                quantized = filters(q)
-            if 0 <= a < TILES:
-                gain(a, True, 0, share)
-            if k < TILES:
-                guard(k)
-            calm = clock[0] not in busy and clock[0] + 4 not in busy
-            if k + 1 < TILES:
-                recompute(k + 1)
-            if 0 <= m < TILES:
-                messages(m)
-                if m % N < N - 1:
-                    waiting.append(m)
-            if 0 <= q < TILES:
-                second_product(q, *quantized)
-            sums_step(k, calm)
-            slot()
+        def step(s):
+            gained, multiplied, sent = s - 1, s - 2, s - 3
+            share = P if gained >= last_chunk else GPSIMD_WORDS
+            if last_chunk <= gained < TILES:
+                gain_on_scalar(gained)
+            elif 0 <= gained < TILES:
+                gain(gained, nc.vector, share, 2 * P)
+            if 0 <= multiplied < TILES:
+                quantized = quantize_f1(multiplied)
+            if 0 <= gained < TILES:
+                gain(gained, nc.gpsimd if gained > 0 else nc.vector, 0, share)
+            if s < TILES:
+                guard(s)
+            calm = clock[0] >= CHUNK_SLOTS[0] and clock[0] not in plan and clock[0] + SLOTS - 1 not in plan
+            if s + 1 < TILES:
+                recompute(s + 1)
+            spare = {TILES - 2: "guard", TILES - 1: "sigmoid"}.get(multiplied)
+            if spare:
+                second_product(multiplied, spare, *quantized)
+            if 0 <= sent < TILES:
+                messages(sent)
+            if 0 <= multiplied < TILES - 2:
+                second_product(multiplied, "filt", *quantized)
+            advance_sums(calm)
+            for unused in range(clock[0], (s + 1) * SLOTS + 2):
+                slot()
 
-        for early in range(-STARTS[0] - 2):
-            slot()
+        for n in range(2 * CHUNKS[0]):
+            sigmoid(n // 2, n % 2, ("sigmoid", "filt")[n % 2])
+        for tl in range(CHUNKS[0]):
+            logarithm(tl)
         recompute(0)
-        for k in range(TILES + 4):
-            step(k)
+        for s in range(TILES + 3):
+            step(s)

import math
from contextlib import ExitStack

import concourse.mybir as mybir
from concourse.masks import make_identity

B, N, G, F, C = 32, 8, 512, 1024, 1024
FLOPS = 2 * B * N * N * (G * F + F * C)

F32 = mybir.dt.float32
BF16 = mybir.dt.bfloat16
I32 = mybir.dt.int32
U32 = mybir.dt.uint32
U8 = mybir.dt.uint8
FP8 = mybir.dt.float8_e4m3fn
FP8X4 = mybir.dt.float8_e4m3fn_x4
ALU = mybir.AluOpType
ACT = mybir.ActivationFunctionType

P = 128
PACK = 4
BANK = 512
TILES = B * N * N // P
QUADS = 4
TERMS = 8
SLOTS = 5

CHUNKS = [6,6,4]
CHUNK_SLOTS = [10,41]
GPSIMD_WORDS = 192
SCALAR_ROWS = 2


def tile_schnetfilterinteraction_kernel(tc, x, dist, mu, gr, w1, gf, w2_bytes, w2_scale, out):
    nc = tc.nc
    with ExitStack() as ctx:
        keep = ctx.enter_context(tc.tile_pool(name="keep", bufs=1))
        work = ctx.enter_context(tc.tile_pool(name="work", bufs=2))
        psum = ctx.enter_context(tc.psum_pool(name="psum", bufs=2))
        ctx.enter_context(tc.manual_schedule())

        gr_sb = keep.tile([P, PACK], BF16, name="gr_sb")
        nc.sync.dma_start(out=gr_sb[:], in_=gr.rearrange("(p t) -> p t", t=PACK))
        mu_sb = keep.tile([P, PACK], BF16, name="mu_sb")
        nc.sync.dma_start(out=mu_sb[:], in_=mu.rearrange("(p t) -> p t", t=PACK))
        dist_sb = keep.tile([P, TILES], BF16, name="dist_sb")
        dist_q = dist.rearrange("b (h q) j -> q b h j", q=QUADS)
        for q in range(QUADS):
            nc.sync.dma_start(out=dist_sb[B * q : B * (q + 1), :].rearrange("p (h j) -> p h j", j=N), in_=dist_q[q])
        w2_scale_sb = keep.tile([P, 2, PACK], F32, name="w2_scale_sb")
        nc.sync.dma_start(out=w2_scale_sb[:], in_=w2_scale.rearrange("(g p t) o -> p g (t o)", p=P, t=PACK))
        w2_rows = w2_bytes.rearrange("(g p t) c -> g p (t c)", p=P, t=PACK)
        w1_rows = w1.rearrange("(p t) f -> p t f", t=PACK)
        w2_raw = [keep.tile([P, PACK * C], U8, name="w2_fp8_bytes%d" % g) for g in range(2)]
        w1_raw = [keep.tile([P, PACK, BANK], BF16, name="w1_raw%d" % g) for g in range(2)]
        nc.sync.dma_start(out=w2_raw[0][:], in_=w2_rows[0])
        for g in range(2):
            nc.sync.dma_start(out=w1_raw[g][:], in_=w1_rows[:, :, g * BANK : (g + 1) * BANK])
        nc.sync.dma_start(out=w2_raw[1][:], in_=w2_rows[1])
        gf_sb = keep.tile([P, 2, PACK], BF16, name="gf_sb")
        nc.sync.dma_start(out=gf_sb[:], in_=gf.rearrange("(g p t) -> p g t", p=P, t=PACK))
        x_sb = keep.tile([P, N * C], BF16, name="x_sb")
        for q in range(QUADS):
            nc.sync.dma_start(out=x_sb[B * q : B * (q + 1), :], in_=x.rearrange("b j c -> b (j c)"))

        ident_bf = keep.tile([P, P], BF16, name="ident_bf")
        make_identity(nc, ident_bf[:])
        ident_f32 = keep.tile([P, P], F32, name="ident_f32")
        make_identity(nc, ident_f32[:])

        tiny = keep.tile([P, 1], F32, name="tiny")
        nc.vector.memset(tiny[:], 2.0**-60)
        pair_terms = keep.tile([P, TILES * TERMS + P], BF16, name="pair_terms")
        nc.vector.memset(pair_terms[:], 1.0)
        gauss_terms = keep.tile([P, PACK, P], BF16, name="gauss_terms")
        nc.vector.memset(gauss_terms[:], 0.0)
        nc.vector.memset(gauss_terms[:, :, 1:3], 1.0)

        gr_abs = keep.tile([P, PACK], F32, name="gr_abs")
        nc.vector.scalar_tensor_tensor(out=gr_abs[:], in0=gr_sb[:], scalar=-1.0, in1=gr_sb[:], op0=ALU.mult, op1=ALU.max)
        gr_log = keep.tile([P, PACK], F32, name="gr_log")
        nc.scalar.activation(out=gr_log[:], in_=gr_abs[:], func=ACT.Ln, bias=tiny[:])
        floor = keep.tile([P, 1], F32, name="floor")
        nc.scalar.activation(out=floor[:], in_=tiny[:], func=ACT.Exp, bias=-42.0)
        w2_wide = [keep.tile([P, PACK, C], BF16, name="w2_wide%d" % g) for g in range(2)]
        for t in range(SCALAR_ROWS):
            nc.scalar.activation(
                out=w2_wide[0][:, t, :],
                in_=w2_raw[0][:, t * C : (t + 1) * C].bitcast(FP8),
                func=ACT.Copy,
                scale=w2_scale_sb[:, 0, t : t + 1],
            )

        pair_term = pair_terms[:, 0 : TILES * TERMS].rearrange("p (a k) -> p a k", k=TERMS)
        mu_sq = keep.tile([P, PACK], F32, name="mu_sq")
        dist_sq = keep.tile([P, TILES], F32, name="dist_sq")
        log_rest = keep.tile([P, PACK], F32, name="log_rest")
        gr_negative = keep.tile([P, PACK], F32, name="gr_negative")
        minus_sign = keep.tile([P, PACK], F32, name="minus_sign")
        nc.vector.tensor_tensor(out=mu_sq[:], in0=mu_sb[:], in1=mu_sb[:], op=ALU.mult)
        nc.vector.tensor_scalar(out=gauss_terms[:, :, 0], in0=mu_sb[:], scalar1=-2.0, scalar2=None, op0=ALU.mult)
        nc.vector.tensor_tensor(out=dist_sq[:], in0=dist_sb[:], in1=dist_sb[:], op=ALU.mult)
        nc.vector.tensor_copy(out=pair_term[:, :, 0], in_=dist_sb[:])
        nc.vector.tensor_scalar(out=gauss_terms[:, :, 5], in0=gr_log[:], scalar1=-0.1, scalar2=None, op0=ALU.mult)
        nc.vector.tensor_copy(out=pair_term[:, :, 1], in_=dist_sq[:])
        nc.vector.scalar_tensor_tensor(
            out=log_rest[:], in0=gr_log[:], scalar=-0.1, in1=gauss_terms[:, :, 5], op0=ALU.mult, op1=ALU.subtract
        )
        nc.vector.tensor_tensor(out=pair_term[:, :, 2], in0=dist_sq[:], in1=pair_term[:, :, 1], op=ALU.subtract)
        nc.vector.tensor_copy(out=gauss_terms[:, :, 6], in_=log_rest[:])
        nc.vector.tensor_scalar(out=gr_negative[:], in0=gr_sb[:], scalar1=0.0, scalar2=2.0, op0=ALU.is_lt, op1=ALU.mult)
        nc.vector.tensor_copy(out=gauss_terms[:, :, 3], in_=mu_sq[:])
        nc.vector.tensor_tensor(out=gauss_terms[:, :, 7], in0=log_rest[:], in1=gauss_terms[:, :, 6], op=ALU.subtract)
        nc.vector.tensor_scalar(out=minus_sign[:], in0=gr_negative[:], scalar1=-1.0, scalar2=None, op0=ALU.add)
        nc.vector.tensor_tensor(out=gauss_terms[:, :, 4], in0=mu_sq[:], in1=gauss_terms[:, :, 3], op=ALU.subtract)

        pair_rows = keep.tile([P, TILES * P], BF16, name="pair_rows")
        gauss_rows = keep.tile([P, PACK * P], BF16, name="gauss_rows")

        def turn_pairs(first, last):
            turned = psum.tile([P, (last - first) * P], BF16, name="turned", tag="sums")
            for a in range(first, last):
                nc.tensor.transpose(
                    turned[:, (a - first) * P : (a - first + 1) * P], pair_terms[:, a * TERMS : a * TERMS + P], ident_bf[:]
                )
            return lambda: nc.vector.tensor_copy(out=pair_rows[:, first * P : last * P], in_=turned[:])

        def turn_gaussians():
            turned = psum.tile([P, PACK * P], BF16, name="turned", tag="guard")
            for t in range(PACK):
                nc.tensor.transpose(turned[:, t * P : (t + 1) * P], gauss_terms[:, t, :], ident_bf[:])
            nc.vector.tensor_copy(out=gauss_rows[:], in_=turned[:])

        r_codes = keep.tile([P, TILES * P], U32, name="r_codes", align_bytes=64)
        r_scales = keep.tile([P, TILES * P], U8, name="r_scales", align_bytes=64)
        r_bf = [keep.tile([P, 4 * BANK], BF16, name="r_bf%d" % n, align_bytes=64) for n in range(TILES // 4)]

        def radial_basis(tl):
            expo = psum.tile([P, PACK, P], F32, name="expo", tag=("sigmoid", "filt")[tl % 2])
            for t in range(PACK):
                nc.tensor.matmul(
                    expo[:, t, :],
                    lhsT=gauss_rows[:, t * P : (t + 1) * P],
                    rhs=pair_rows[:, tl * P : (tl + 1) * P],
                    start=True,
                    stop=True,
                )
            place = slice(tl % 4 * BANK, (tl % 4 + 1) * BANK)
            nc.scalar.activation(
                out=r_bf[tl // 4][:, place].rearrange("p (n t) -> p n t", t=PACK),
                in_=expo[:].rearrange("p t n -> p n t"),
                func=ACT.Exp,
                scale=-10.0,
            )

        def quantize_r(n):
            cols = slice(n * BANK, (n + 1) * BANK)
            nc.vector.quantize_mx(out=r_codes[:, cols].bitcast(FP8X4), scales=r_scales[:, cols], in_=r_bf[n][:])

        cutoff = keep.tile([P, TILES], F32, name="cutoff")
        turns = keep.tile([P, TILES], F32, name="turns")
        whole = keep.tile([P, TILES], I32, name="whole")
        angle = keep.tile([P, TILES], F32, name="angle")
        angle_sq = keep.tile([P, TILES], F32, name="angle_sq")
        sine = keep.tile([P, TILES], F32, name="sine")

        def horner(k):
            factor = angle_sq if k > 0 else angle
            return lambda: nc.vector.scalar_tensor_tensor(
                out=sine[:], in0=sine[:], scalar=(-1.0) ** k / math.factorial(2 * k + 1), in1=factor[:], op0=ALU.add, op1=ALU.mult
            )

        cutoff_steps = [
            lambda: nc.vector.tensor_scalar(out=turns[:], in0=dist_sb[:], scalar1=0.1, scalar2=None, op0=ALU.mult),
            lambda: nc.vector.tensor_copy(out=whole[:], in_=turns[:]),
            lambda: nc.vector.tensor_tensor(out=turns[:], in0=turns[:], in1=whole[:], op=ALU.subtract),
            lambda: nc.vector.scalar_tensor_tensor(
                out=turns[:], in0=turns[:], scalar=-1.0, in1=turns[:], op0=ALU.mult, op1=ALU.max
            ),
            lambda: nc.vector.tensor_scalar(
                out=angle[:], in0=turns[:], scalar1=-math.pi, scalar2=math.pi / 2, op0=ALU.mult, op1=ALU.add
            ),
            lambda: nc.vector.tensor_tensor(out=angle_sq[:], in0=angle[:], in1=angle[:], op=ALU.mult),
            lambda: nc.vector.tensor_scalar(
                out=sine[:], in0=angle_sq[:], scalar1=-1.0 / math.factorial(15), scalar2=None, op0=ALU.mult
            ),
        ]
        cutoff_steps.extend(horner(k) for k in range(6, -1, -1))
        cutoff_steps.append(
            lambda: nc.vector.scalar_tensor_tensor(
                out=cutoff[:], in0=sine[:], scalar=1.0 / math.sqrt(N), in1=sine[:], op0=ALU.mult, op1=ALU.mult
            )
        )

        w1_codes = keep.tile([P, F], U32, name="w1_codes", align_bytes=64)
        w1_scales = keep.tile([P, F], U8, name="w1_scales", align_bytes=64)
        w2_codes = keep.tile([P, 2, C], U32, name="w2_codes", align_bytes=64)
        w2_scales = keep.tile([P, 2, C], U8, name="w2_scales", align_bytes=64)
        minus_gf = keep.tile([P, 2, P, PACK], F32, name="minus_gf")

        def sign_w1(g):
            signed = work.tile([P, PACK, BANK], BF16, name="signed", tag="signed")
            for j in range(PACK):
                nc.vector.tensor_scalar(
                    out=signed[:, j, :], in0=w1_raw[g][:, j, :], scalar1=minus_sign[:, j : j + 1], scalar2=None, op0=ALU.mult
                )
            return signed

        def group_w1(signed):
            grouped = work.tile([P, PACK * BANK], BF16, name="grouped", tag="grouped", align_bytes=64)
            nc.vector.tensor_copy(
                out=grouped[:].rearrange("p (t a e j) -> p a t e j", t=PACK, e=2, j=PACK),
                in_=signed[:].rearrange("p j (a e t) -> p a t e j", t=PACK, e=2),
            )
            return grouped

        def quantize_w1(g, grouped):
            cols = slice(g * BANK, (g + 1) * BANK)
            nc.vector.quantize_mx(out=w1_codes[:, cols].bitcast(FP8X4), scales=w1_scales[:, cols], in_=grouped[:])

        def widen_w2(g, t):
            nc.vector.tensor_scalar(
                out=w2_wide[g][:, t, :],
                in0=w2_raw[g][:, t * C : (t + 1) * C].bitcast(FP8),
                scalar1=w2_scale_sb[:, g, t : t + 1],
                scalar2=None,
                op0=ALU.mult,
            )

        def group_w2(g, half):
            grouped = work.tile([P, PACK * BANK], BF16, name="grouped", tag="grouped", align_bytes=64)
            nc.vector.tensor_copy(
                out=grouped[:].rearrange("p (a e t) -> p a t e", t=PACK, e=4),
                in_=w2_wide[g][:, :, half * BANK : (half + 1) * BANK].rearrange("p t (a e) -> p a t e", e=4),
            )
            return grouped

        def quantize_w2(g, half, grouped):
            cols = slice(half * BANK, (half + 1) * BANK)
            nc.vector.quantize_mx(out=w2_codes[:, g, cols].bitcast(FP8X4), scales=w2_scales[:, g, cols], in_=grouped[:])

        turn_pairs(0, 4)()
        copy_pairs = turn_pairs(4, 8)
        turn_gaussians()
        copy_pairs()
        radial_basis(0)
        radial_basis(1)
        copy_pairs = turn_pairs(8, TILES)
        signed = sign_w1(0)
        copy_pairs()
        for tl in range(2, TILES):
            radial_basis(tl)

        long_steps = []
        grouped = {}
        long_steps.append(lambda: grouped.setdefault("w1a", group_w1(signed)))
        long_steps.append(lambda: grouped.setdefault("signed", sign_w1(1)))
        long_steps.append(lambda: quantize_w1(0, grouped["w1a"]))
        long_steps.append(lambda: grouped.setdefault("w1b", group_w1(grouped["signed"])))
        long_steps.append(lambda: quantize_r(0))
        long_steps.append(lambda: quantize_w1(1, grouped["w1b"]))
        for step_no, long_step in enumerate(long_steps):
            cutoff_steps[step_no]()
            long_step()
        cutoff_steps[6]()
        for t in range(SCALAR_ROWS, PACK):
            widen_w2(0, t)
        quantize_r(1)
        for t in range(PACK):
            cutoff_steps[7 + t]()
            widen_w2(1, t)
        between = [
            lambda: quantize_r(2),
            lambda: quantize_r(3),
            lambda: nc.vector.tensor_scalar(
                out=minus_gf[:], in0=gf_sb[:].unsqueeze(2).to_broadcast([P, 2, P, PACK]), scalar1=-1.0, scalar2=None, op0=ALU.mult
            ),
            cutoff_steps[14],
        ]
        for quarter in range(4):
            half, g = divmod(quarter, 2)
            ready = group_w2(g, half)
            if quarter < 3:
                cutoff_steps[11 + quarter]()
            between[quarter]()
            quantize_w2(g, half, ready)

        logs, again, soft, f1, filt, msg, sums, back = {}, {}, {}, {}, {}, {}, {}, {}

        def minus_h(tl, g, tag):
            bank = psum.tile([P, PACK, P], F32, name="minus_h", tag=tag)
            pairs = slice(tl * P, (tl + 1) * P)
            for t in range(PACK):
                cols = slice(g * BANK + t * P, g * BANK + (t + 1) * P)
                nc.tensor.matmul_mx(
                    out=bank[:, t, :],
                    lhsT=w1_codes[:, cols].bitcast(FP8X4),
                    lhsT_scale=w1_scales[:, cols],
                    rhs=r_codes[:, pairs].bitcast(FP8X4),
                    rhs_scale=r_scales[:, pairs],
                    start=True,
                    stop=True,
                )
            return bank[:].rearrange("p t n -> p n t")

        def sigmoid(tl, g, tag):
            if g == 0:
                logs[tl] = work.tile([P, 2, P, PACK], F32, name="logs", tag="logs", bufs=CHUNKS[0] + CHUNKS[1])
            nc.scalar.activation(out=logs[tl][:, g, :, :], in_=minus_h(tl, g, tag), func=ACT.Sigmoid)

        def logarithm(tl):
            flat = logs[tl][:].rearrange("p g n t -> p (g n t)")
            nc.scalar.activation(out=flat, in_=flat, func=ACT.Ln, scale=2.0, bias=floor[:])

        def recompute(tl):
            again[tl] = []
            for g in range(2):
                again[tl].append(minus_h(tl, g, "guard"))
                slot()

        def guard(tl):
            soft[tl] = work.tile([P, 2, P, PACK], F32, name="soft", tag="soft", bufs=3)
            for g in range(2):
                nc.vector.scalar_tensor_tensor(
                    out=soft[tl][:, g, :, :],
                    in0=again[tl][g],
                    scalar=math.log(2.0),
                    in1=logs[tl][:, g, :, :],
                    op0=ALU.add,
                    op1=ALU.min,
                )

        def gain(tl, engine, first, last):
            part = work.tile(
                [P, (last - first) * PACK], BF16, name="f1", tag="f1_from%d" % min(first, 1), align_bytes=64,
                bufs=1 if first == 0 else 3,
            )
            f1.setdefault(tl, []).append((first, last, part))
            cols = slice(first * PACK, last * PACK)
            engine.tensor_tensor(
                out=part[:],
                in0=soft[tl][:].rearrange("p g n t -> p (g n t)")[:, cols],
                in1=minus_gf[:].rearrange("p g n t -> p (g n t)")[:, cols],
                op=ALU.mult,
            )

        def gain_on_scalar(tl):
            planes = work.tile([P, PACK, P], BF16, name="planes", tag="planes")
            for t in range(PACK):
                nc.scalar.activation(
                    out=planes[:, t, :], in_=soft[tl][:, 1, :, t], func=ACT.Copy, scale=minus_gf[:, 1, 0, t : t + 1]
                )
            part = work.tile([P, BANK], BF16, name="f1", tag="f1_from1", align_bytes=64, bufs=3)
            f1.setdefault(tl, []).append((P, 2 * P, part))
            nc.scalar.copy(out=part[:].rearrange("p (n t) -> p n t", t=PACK), in_=planes[:].rearrange("p t n -> p n t"))

        def quantize_f1(tl):
            codes = work.tile([P, 2 * P], U32, name="f1_codes", tag="f1_codes", align_bytes=64, bufs=3)
            scales = work.tile([P, 2 * P], U8, name="f1_scales", tag="f1_scales", align_bytes=64, bufs=3)
            for first, last, part in f1[tl]:
                cuts = [first, P, last] if first < P < last else [first, last]
                for lo, hi in zip(cuts, cuts[1:]):
                    nc.vector.quantize_mx(
                        out=codes[:, lo:hi].bitcast(FP8X4),
                        scales=scales[:, lo:hi],
                        in_=part[:, (lo - first) * PACK : (hi - first) * PACK],
                    )
            return codes, scales

        def second_product(tl, tag, codes, scales):
            filt[tl] = []
            for half in range(2):
                cols = slice(half * BANK, (half + 1) * BANK)
                bank = psum.tile([P, BANK], F32, name="filt", tag=tag)
                for g in range(2):
                    nc.tensor.matmul_mx(
                        out=bank[:],
                        lhsT=codes[:, g * P : (g + 1) * P].bitcast(FP8X4),
                        lhsT_scale=scales[:, g * P : (g + 1) * P],
                        rhs=w2_codes[:, g, cols].bitcast(FP8X4),
                        rhs_scale=w2_scales[:, g, cols],
                        start=(g == 0),
                        stop=(g == 1),
                    )
                filt[tl].append(bank)
                slot()

        def messages(tl):
            msg[tl] = []
            for half in range(2):
                part = work.tile([P, BANK], F32, name="msg", tag="msg", bufs=16)
                first = tl % N * C + half * BANK
                nc.vector.scalar_tensor_tensor(
                    out=part[:],
                    in0=filt[tl][half][:],
                    scalar=cutoff[:, tl : tl + 1],
                    in1=x_sb[:, first : first + BANK],
                    op0=ALU.mult,
                    op1=ALU.mult,
                )
                msg[tl].append(part)

        added = [N - 1, N - 1]

        def add_up(tl):
            h, j = divmod(tl, N)
            if j == 0:
                sums[h] = [psum.tile([P, BANK], F32, name="sums", tag="sums") for half in range(2)]
            for half in range(2):
                for a in range(BANK // P):
                    nc.tensor.matmul(
                        sums[h][half][:, a * P : (a + 1) * P],
                        lhsT=msg[tl][half][:, a * P : (a + 1) * P],
                        rhs=ident_f32[:],
                        is_transpose=True,
                        start=(j == 0 and a == 0),
                        stop=(j == added[h] - 1 and a == BANK // P - 1),
                    )

        def turn_back(h):
            parked = [work.tile([P, BANK], F32, name="parked", tag="parked") for half in range(2)]
            for half in range(2):
                nc.scalar.copy(out=parked[half][:], in_=sums[h][half][:])
            back[h] = []
            for half in range(2):
                bank = psum.tile([P, BANK], F32, name="back", tag="sums")
                for a in range(BANK // P):
                    nc.tensor.transpose(bank[:, a * P : (a + 1) * P], parked[half][:, a * P : (a + 1) * P], ident_f32[:])
                back[h].append(bank)

        out_q = out.rearrange("b (h q) c -> h q b c", q=QUADS)

        def add_on_vector(tl):
            h, j = divmod(tl, N)
            for half in range(2):
                total = work.tile([P, BANK], F32, name="total", tag="total")
                nc.vector.tensor_tensor(out=total[:], in0=back[h][half][:], in1=msg[tl][half][:], op=ALU.add)
                back[h][half] = total
                if j == N - 1:
                    for q in range(QUADS):
                        queue = nc.scalar if tl == TILES - 1 and q % 2 else nc.sync
                        queue.dma_start(
                            out=out_q[h, q][:, half * BANK : (half + 1) * BANK], in_=total[B * q : B * (q + 1), :]
                        )

        plan = {}
        first = CHUNKS[0]
        for size, start, tags in zip(CHUNKS[1:], CHUNK_SLOTS, (("sigmoid", "sums"), ("sigmoid", "sigmoid"))):
            for n in range(2 * size):
                plan[start + n] = (first + n // 2, n % 2, tags[n % 2], range(first, first + size) if n == 2 * size - 1 else [])
            first = first + size
        clock = [0]

        def slot():
            if clock[0] in plan:
                tl, g, tag, finished = plan[clock[0]]
                sigmoid(tl, g, tag)
                for done in finished:
                    logarithm(done)
            clock[0] = clock[0] + 1

        next_sum = [0]
        last_chunk = TILES - CHUNKS[-1]

        def advance_sums(calm):
            h, j = divmod(next_sum[0], N)
            if j >= added[h] and h in back and next_sum[0] in msg:
                add_on_vector(next_sum[0])
                next_sum[0] = next_sum[0] + 1
            elif j == added[h] and h not in back:
                turn_back(h)
            if calm:
                h, j = divmod(next_sum[0], N)
                for tl in range(next_sum[0], N * h + min(j + 2, added[min(h, 1)])):
                    if tl in msg:
                        add_up(tl)
                        next_sum[0] = tl + 1
            if next_sum[0] == N + added[1] and 1 not in back:
                turn_back(1)

        def step(s):
            gained, multiplied, sent = s - 1, s - 2, s - 3
            share = P if gained >= last_chunk else GPSIMD_WORDS
            if last_chunk <= gained < TILES:
                gain_on_scalar(gained)
            elif 0 <= gained < TILES:
                gain(gained, nc.vector, share, 2 * P)
            if 0 <= multiplied < TILES:
                quantized = quantize_f1(multiplied)
            if 0 <= gained < TILES:
                gain(gained, nc.gpsimd if gained > 0 else nc.vector, 0, share)
            if s < TILES:
                guard(s)
            calm = clock[0] >= CHUNK_SLOTS[0] and clock[0] not in plan and clock[0] + SLOTS - 1 not in plan
            if s + 1 < TILES:
                recompute(s + 1)
            spare = {TILES - 2: "guard", TILES - 1: "sigmoid"}.get(multiplied)
            if spare:
                second_product(multiplied, spare, *quantized)
            if 0 <= sent < TILES:
                messages(sent)
            if 0 <= multiplied < TILES - 2:
                second_product(multiplied, "filt", *quantized)
            advance_sums(calm)
            for unused in range(clock[0], (s + 1) * SLOTS + 2):
                slot()

        for n in range(2 * CHUNKS[0]):
            sigmoid(n // 2, n % 2, ("sigmoid", "filt")[n % 2])
        for tl in range(CHUNKS[0]):
            logarithm(tl)
        recompute(0)
        for s in range(TILES + 3):
            step(s)
